import numpy as np
import ml_dtypes


def mxq(x, axis, fmt="e4m3"):
    dtype, down = {"e4m3": (ml_dtypes.float8_e4m3fn, 7), "e5m2": (ml_dtypes.float8_e5m2, 14)}[fmt]
    v = np.moveaxis(np.asarray(x, np.float32).astype(ml_dtypes.bfloat16).astype(np.float64), axis, -1)
    blocks = v.reshape(v.shape[:-1] + (-1, 32))
    amax = np.abs(blocks).max(-1, keepdims=True)
    byte = np.maximum(np.where(amax > 0, np.frexp(amax)[1] - 1 + 127, 0) - down, 1)
    scale = np.exp2(byte - 127.0)
    codes = (blocks / scale).astype(np.float32).astype(dtype).astype(np.float64)
    return np.moveaxis((codes * scale).reshape(v.shape), -1, axis)


WIDE = False


def mx_kscale(k):
    if not WIDE:
        return np.ones(k)
    levels = np.array([30, -30])
    if k % 512:
        return np.exp2(np.random.permutation(np.resize(levels, k // 32))).repeat(32)
    a = np.empty((k // 512, 16))
    for p in range(k // 512):
        a[p, :8] = np.random.permutation(np.resize(levels, 8))
        for g in range(8):
            far = levels[np.abs(levels - a[p, g]) >= 10]
            a[p, g + 8] = far[np.random.randint(len(far))]
    return np.exp2(a.ravel()).repeat(32)


def f64(x):
    return np.asarray(x).astype(np.float64)


def striped(idx):
    return np.tile(np.asarray(idx).reshape(-1, 16).T, (8, 1)).astype(np.uint16)


def unstriped(offs):
    return offs[:16].T.reshape(-1).astype(np.int64)


def striped8(idx):
    return np.asarray(idx).reshape(8, -1, 16).transpose(0, 2, 1).reshape(128, -1).astype(np.uint16)


def unstriped8(offs):
    return offs.reshape(8, 16, -1).transpose(0, 2, 1).reshape(8, -1).astype(np.int64)


def pick8(x, idx, run):
    r = np.arange(len(x))
    return x[r[:, None], idx[r % (8 * run) // run]]


E2M1 = np.array([0.0, 0.5, 1.0, 1.5, 2.0, 3.0, 4.0, 6.0, -0.0, -0.5, -1.0, -1.5, -2.0, -3.0, -4.0, -6.0])


def pack_weight(w, fmt):
    k, n = w.shape
    w = f64(np.asarray(w, np.float32).astype(ml_dtypes.bfloat16)).reshape(k // 32, 32, n)
    amax = np.abs(w).max(1)
    if fmt in ("e4m3", "e5m2"):
        byte = np.frexp(amax)[1] - 1 + 127 - (7 if fmt == "e4m3" else 14)
    else:
        mant, ex = np.frexp(amax / 6.0)
        byte = np.where(mant > 0.5, ex, ex - 1) + 127
    byte = np.clip(np.where(amax > 0, byte, 1), 1, 254)
    scaled = (w * np.exp2(127.0 - byte)[:, None, :]).reshape(k, n).astype(np.float32)
    by_word = np.ascontiguousarray(scaled.reshape(k // 512, 128, 4, n).transpose(0, 1, 3, 2))
    if fmt in ("e4m3", "e5m2"):
        words = by_word.astype(ml_dtypes.float8_e4m3fn if fmt == "e4m3" else ml_dtypes.float8_e5m2).view(np.uint8)
    else:
        c = by_word.astype(ml_dtypes.float4_e2m1fn).view(np.uint8) & 0xF
        words = (c[..., 0::2] | (c[..., 1::2] << 4)).reshape(k // 512, 128, 2 * n)
    return np.ascontiguousarray(words), np.ascontiguousarray(byte.astype(np.uint8).reshape(k // 512, 16, n))


def unpack_weight(words, scales, fmt):
    g, _, n = scales.shape
    words = np.ascontiguousarray(words).reshape(g, 128, n, -1)
    if fmt in ("e4m3", "e5m2"):
        vals = words.view(ml_dtypes.float8_e4m3fn if fmt == "e4m3" else ml_dtypes.float8_e5m2).astype(np.float64)
    else:
        nib = np.empty((g, 128, n, 4), np.uint8)
        nib[..., 0::2] = words & 0xF
        nib[..., 1::2] = words >> 4
        vals = E2M1[nib]
    vals = vals * np.repeat(np.exp2(scales.astype(np.float64) - 127.0), 8, axis=1)[..., None]
    return vals.transpose(0, 1, 3, 2).reshape(g * 512, n)


K, T, J, R, C, O, N, S, E = 512, 1024, 256, 512, 512, 128, 256, 1024, 1024


def setup_inputs():
    n = np.random.standard_normal
    idx = np.random.permutation(T)[:J]
    idx2 = np.stack([np.random.permutation(C)[:J] for _ in range(8)])
    idx3 = np.random.permutation(C)[:J]
    idx4 = np.random.permutation(J)[:O]
    idx5 = np.random.permutation(J)[:O]
    idx6 = np.random.permutation(S)[:N]
    idx7 = np.random.permutation(E)[:O]
    fk = mx_kscale(K)
    fr = mx_kscale(R)
    xtp = pack_weight(n((K, T)) / fk[:, None], "e2m1")
    wp = pack_weight(n((K, R)) * 1 / np.sqrt(K) * fk[:, None] * fr, "e5m2")
    w2p = pack_weight(n((K, R)) * 1 / np.sqrt(K) * fk[:, None] * fr, "e4m3")
    vsp = pack_weight(n((R, S)) * 1 / np.sqrt(R) / fr[:, None], "e4m3")
    return {
        "xt_words": xtp[0],
        "xt_scales": xtp[1],
        "w_words": wp[0],
        "w_scales": wp[1],
        "w2_words": w2p[0],
        "w2_scales": w2p[1],
        "sa": (np.random.uniform(0.5, 1.6, (R, 1))).astype(np.float32),
        "sb": (np.random.uniform(0.5, 1.6, (R, 1))).astype(np.float32),
        "vs_words": vsp[0],
        "vs_scales": vsp[1],
        "offs": striped(idx),
        "offs2": striped8(idx2),
        "offs3": striped(idx3),
        "offs4": striped(idx4),
        "offs5": striped(idx5),
        "offs6": striped(idx6),
        "offs7": striped(idx7),
    }


def reference(xt_words, xt_scales, w_words, w_scales, w2_words, w2_scales, sa, sb, vs_words, vs_scales, offs, offs2, offs3, offs4, offs5, offs6, offs7):
    idx = unstriped(offs)
    idx2 = unstriped8(offs2)
    idx3 = unstriped(offs3)
    idx4 = unstriped(offs4)
    idx5 = unstriped(offs5)
    idx6 = unstriped(offs6)
    idx7 = unstriped(offs7)
    xtu = unpack_weight(xt_words, xt_scales, "e2m1")
    wu = unpack_weight(w_words, w_scales, "e5m2")
    w2u = unpack_weight(w2_words, w2_scales, "e4m3")
    vsu = unpack_weight(vs_words, vs_scales, "e4m3")
    xtidxg = xtu[:, idx]
    a = wu.T @ xtidxg
    b = w2u.T @ xtidxg
    pw = np.zeros((R, C))
    pw[np.arange(R)[:, None], idx2[np.arange(R) % 512 // 64]] = a
    rb = np.maximum(pw[:, idx3] * f64(sa), b)
    hid = np.abs(rb[:, idx4] - rb[:, idx5] * f64(sb))
    vsidx6g = vsu[:, idx6]
    hidq = mxq(hid, 0, "e5m2")
    p = vsidx6g.T @ hidq
    y = np.zeros((N, E))
    y[:, idx7] = p
    return y

@@ -1,0 +1,225 @@
+from contextlib import ExitStack
+
+import concourse.mybir as mybir
+
+K, T, J, R, C, O, N, S, E = 512, 1024, 256, 512, 512, 128, 256, 1024, 1024
+FLOPS = 2 * (2 * K * R * J + R * N * O)
+
+F32 = mybir.dt.float32
+BF16 = mybir.dt.bfloat16
+I32 = mybir.dt.int32
+U32 = mybir.dt.uint32
+U16 = mybir.dt.uint16
+U8 = mybir.dt.uint8
+E2M1 = mybir.dt.float4_e2m1fn_x4
+E4M3 = mybir.dt.float8_e4m3fn_x4
+E5M2 = mybir.dt.float8_e5m2_x4
+ACT = mybir.ActivationFunctionType
+ALU = mybir.AluOpType
+
+P = 128
+PACK = 4
+QUADS = 4
+QROWS = 32
+HALF = J // 2
+
+
+def load_plane(nc, queues, plane, scales):
+    rows = scales[0].bitcast(I32)
+    nc.vector.memset(plane[:].bitcast(I32), 0)
+    for q in range(QUADS):
+        queues[q].dma_start(
+            out=plane[QROWS * q : QROWS * q + PACK, :].bitcast(I32), in_=rows[PACK * q : PACK * (q + 1), :]
+        )
+
+
+def tile_list_ownanswer_twow_store_scattered_kernel(
+    tc, xt_words, xt_scales, w_words, w_scales, w2_words, w2_scales, sa, sb, vs_words, vs_scales,
+    offs, offs2, offs3, offs4, offs5, offs6, offs7, out,
+):
+    nc = tc.nc
+    with ExitStack() as ctx:
+        lists = ctx.enter_context(tc.tile_pool(name="lists", bufs=1))
+        work = ctx.enter_context(tc.tile_pool(name="work", bufs=1))
+        psum = ctx.enter_context(tc.psum_pool(name="psum", bufs=1))
+
+        def tile(shape, dtype, name, tag=None):
+            return work.tile(shape, dtype, name=name, tag=tag or name, align_bytes=64)
+
+        def load_list(src, name):
+            dst = lists.tile(list(src.shape), U16, name=name)
+            nc.sync.dma_start(dst[:], src)
+            return dst
+
+        def load_words(queue, src, cols, dtype, name):
+            dst = tile([P, cols], dtype, name)
+            queue.dma_start(out=dst[:].bitcast(I32), in_=src.bitcast(I32))
+            return dst
+
+        ws_stage = tile([PACK, QUADS, R // 4], I32, "ws_stage")
+        nc.sync.dma_start(out=ws_stage[:], in_=w_scales[0].bitcast(I32).rearrange("(q r) c -> r q c", r=PACK))
+        x_words = load_words(nc.scalar, xt_words[0], T, U16, "x_words")
+        x_plane = tile([P, T], U8, "x_plane")
+        load_plane(nc, [nc.sync, nc.sync, nc.scalar, nc.scalar], x_plane, xt_scales)
+        l1 = load_list(offs, "l1")
+        w_raw = load_words(nc.scalar, w_words[0].rearrange("p c t -> p (c t)"), R, I32, "w_raw")
+        w_plane = tile([P, R], U8, "w_plane")
+        nc.vector.memset(w_plane[:].bitcast(I32), 0)
+        board = [tile([P, C], F32, "board%d" % t) for t in range(PACK)]
+        for t in range(PACK):
+            nc.vector.memset(board[t][:], 0.0)
+        l2 = load_list(offs2, "l2")
+        w2s_stage = tile([PACK, QUADS, R // 4], I32, "w2s_stage")
+        nc.sync.dma_start(out=w2s_stage[:], in_=w2_scales[0].bitcast(I32).rearrange("(q r) c -> r q c", r=PACK))
+        w2_raw = load_words(nc.sync, w2_words[0].rearrange("p c t -> p (c t)"), R, I32, "w2_raw")
+        w2_plane = tile([P, R], U8, "w2_plane")
+        nc.vector.memset(w2_plane[:].bitcast(I32), 0)
+        l5 = load_list(offs5, "l5")
+        sb_t = tile([P, PACK], F32, "sb_t")
+        nc.sync.dma_start(out=sb_t[:], in_=sb.rearrange("(p t) o -> p (t o)", t=PACK))
+        l3 = load_list(offs3, "l3")
+        sa_t = tile([P, PACK], F32, "sa_t")
+        nc.sync.dma_start(out=sa_t[:], in_=sa.rearrange("(p t) o -> p (t o)", t=PACK))
+        l4 = load_list(offs4, "l4")
+        v_words = load_words(nc.sync, vs_words[0].rearrange("p c t -> p (c t)"), S, U32, "v_words")
+        l6 = load_list(offs6, "l6")
+        v_plane = tile([P, S], U8, "v_plane")
+        load_plane(nc, [nc.sync] * QUADS, v_plane, vs_scales)
+        l7 = load_list(offs7, "l7")
+
+        for q in range(QUADS):
+            nc.vector.tensor_copy(out=w_plane[QROWS * q : QROWS * q + PACK, :].bitcast(I32), in_=ws_stage[:, q, :])
+
+        def deal_scales(plane, name):
+            scales = tile([P, PACK, P], U8, name)
+            nc.vector.tensor_copy(out=scales[:], in_=plane[:].rearrange("p (m t) -> p t m", t=PACK))
+            return scales
+
+        def deal_words(raw, t0, t1, name):
+            words = tile([P, t1 - t0, P], I32, name)
+            nc.vector.tensor_copy(
+                out=words[:].rearrange("p t m -> p m t"),
+                in_=raw[:].rearrange("p (m t) -> p m t", t=PACK)[:, :, t0:t1],
+            )
+            return words
+
+        xg_words = tile([P, J], U16, "xg_words")
+        xg_scales = tile([P, J], U8, "xg_scales")
+
+        def pick_tokens(j0, j1):
+            cols = l1[:, j0 // 16 : j1 // 16]
+            nc.vector.tensor_copy(out=xg_words[:, j0:j1], in_=x_words[:].indirect(cols))
+            nc.vector.tensor_copy(out=xg_scales[:, j0:j1], in_=x_plane[:].indirect(cols))
+
+        def stage1(dst, words, scales, fmt, j0, j1):
+            nc.tensor.matmul_mx(
+                out=dst, lhsT=words.bitcast(fmt), lhsT_scale=scales,
+                rhs=xg_words[:, j0:j1].bitcast(E2M1), rhs_scale=xg_scales[:, j0:j1], start=True, stop=True,
+            )
+
+        def put(t, src, j0, j1):
+            nc.scalar.activation(out=board[t][:].indirect(l2[:, j0 // 16 : j1 // 16]), in_=src, func=ACT.Copy)
+
+        w_sc = deal_scales(w_plane, "w_sc")
+        pick_tokens(0, HALF)
+        wa_words = deal_words(w_raw, 0, 2, "wa_words")
+        first = []
+        for t in range(2):
+            bank = psum.tile([P, HALF], F32, name="a_first%d" % t)
+            stage1(bank[:], wa_words[:, t, :], w_sc[:, t, :], E5M2, 0, HALF)
+            a_sb = tile([P, HALF], F32, "a_first_sb%d" % t)
+            nc.scalar.activation(out=a_sb[:], in_=bank[:], func=ACT.Copy)
+            first.append(a_sb)
+        for t in range(2):
+            put(t, first[t][:], 0, HALF)
+
+        pick_tokens(HALF, J)
+        bank_b = psum.tile([P, 2, HALF], F32, name="a_second")
+        for t in range(2):
+            stage1(bank_b[:, t, :], wa_words[:, t, :], w_sc[:, t, :], E5M2, HALF, J)
+        wb_words = deal_words(w_raw, 2, 4, "wb_words")
+        a_second = tile([P, 2, HALF], F32, "a_second_sb")
+        nc.vector.tensor_copy(out=a_second[:], in_=bank_b[:])
+        for t in range(2):
+            put(t, a_second[:, t, :], HALF, J)
+        bank_c = psum.tile([P, 2, J], F32, name="a_rest")
+        for t in range(2):
+            stage1(bank_c[:, t, :], wb_words[:, t, :], w_sc[:, 2 + t, :], E5M2, 0, J)
+
+        for q in range(QUADS):
+            nc.vector.tensor_copy(out=w2_plane[QROWS * q : QROWS * q + PACK, :].bitcast(I32), in_=w2s_stage[:, q, :])
+        w2_sc = deal_scales(w2_plane, "w2_sc")
+        w2d_words = deal_words(w2_raw, 0, PACK, "w2d_words")
+        b_bank = [psum.tile([P, 2, J], F32, name="b%d" % u) for u in range(2)]
+        for t in range(PACK):
+            stage1(b_bank[t // 2][:, t % 2, :], w2d_words[:, t, :], w2_sc[:, t, :], E4M3, 0, J)
+
+        page = [tile([P, E], F32, "page0", "w2_plane"), tile([P, E], F32, "page1", "w2_raw")]
+        for h in range(N // P):
+            nc.vector.memset(page[h][:], 0.0)
+        rb = [tile([P, J], F32, "rb%d" % t) for t in range(PACK)]
+        hid = tile([P, O, PACK], BF16, "hid")
+
+        def fetch(t, tag):
+            q = tile([P, J], F32, "fetched%d" % t, tag)
+            nc.scalar.activation(out=q[:], in_=board[t][:].indirect(l3[:]), func=ACT.Copy, scale=sa_t[:, t : t + 1])
+            return q
+
+        def larger(t, q):
+            nc.vector.tensor_tensor(out=rb[t][:], in0=b_bank[t // 2][:, t % 2, :], in1=q[:], op=ALU.max)
+
+        def differ(t, dst):
+            y = tile([P, O], F32, "second%d" % t)
+            nc.scalar.activation(out=y[:], in_=rb[t][:].indirect(l5[:]), func=ACT.Copy, scale=sb_t[:, t : t + 1])
+            nc.vector.tensor_tensor(out=dst, in0=rb[t][:].indirect(l4[:]), in1=y[:], op=ALU.subtract)
+
+        q0 = fetch(0, None)
+        q1 = fetch(1, None)
+        a2 = tile([P, J], F32, "a2_sb", "board0")
+        nc.vector.tensor_copy(out=a2[:], in_=bank_c[:, 0, :])
+        put(2, a2[:], 0, J)
+        larger(0, q0)
+        larger(1, q1)
+        a3 = tile([P, J], F32, "a3_sb", "fetched1")
+        nc.vector.tensor_copy(out=a3[:], in_=bank_c[:, 1, :])
+
+        vg_words = tile([P, N], U32, "vg_words")
+        vg_scales = tile([P, N], U8, "vg_scales")
+        nc.vector.tensor_copy(out=vg_words[:], in_=v_words[:].indirect(l6[:]))
+        nc.vector.tensor_copy(out=vg_scales[:], in_=v_plane[:].indirect(l6[:]))
+
+        diff_low = tile([P, 2, O], F32, "diff_low", "v_plane")
+        differ(0, diff_low[:, 0, :])
+        differ(1, diff_low[:, 1, :])
+        put(3, a3[:], 0, J)
+        low = diff_low[:].rearrange("p t o -> p o t")
+        nc.vector.scalar_tensor_tensor(out=hid[:, :, 0:2], in0=low, scalar=-1.0, in1=low, op0=ALU.mult, op1=ALU.max)
+
+        q2 = fetch(2, "second0")
+        q3 = fetch(3, "second1")
+        larger(2, q2)
+        larger(3, q3)
+        diff_high = tile([P, 2, O], F32, "diff_high")
+        differ(2, diff_high[:, 0, :])
+        differ(3, diff_high[:, 1, :])
+        nc.scalar.activation(out=hid[:, :, 2:4], in_=diff_high[:].rearrange("p t o -> p o t"), func=ACT.Abs)
+
+        h_words = tile([P, O], U32, "h_words")
+        h_scales = tile([P, O], U8, "h_scales")
+        nc.vector.quantize_mx(out=h_words[:].bitcast(E5M2), scales=h_scales[:], in_=hid[:].rearrange("p o t -> p (o t)"))
+
+        banks, p_sb = [], []
+        for h in range(N // P):
+            bank = psum.tile([P, O], F32, name="p%d" % h)
+            nc.tensor.matmul_mx(
+                out=bank[:], lhsT=vg_words[:, h * P : (h + 1) * P].bitcast(E4M3), lhsT_scale=vg_scales[:, h * P : (h + 1) * P],
+                rhs=h_words[:].bitcast(E5M2), rhs_scale=h_scales[:], start=True, stop=True,
+            )
+            banks.append(bank)
+            p_sb.append(tile([P, O], F32, "p_sb%d" % h))
+        nc.scalar.activation(out=p_sb[0][:], in_=banks[0][:], func=ACT.Copy)
+        nc.vector.tensor_copy(out=p_sb[1][:], in_=banks[1][:])
+        nc.vector.tensor_copy(out=page[0][:].indirect(l7[:]), in_=p_sb[0][:])
+        nc.scalar.activation(out=page[1][:].indirect(l7[:]), in_=p_sb[1][:], func=ACT.Copy)
+        for h in range(N // P):
+            nc.sync.dma_start(out=out[h * P : (h + 1) * P, :], in_=page[h][:])

@@ -168,14 +168,15 @@ def tile_list_ownanswer_twow_store_scattered_kernel(
         def larger(t, q):
             nc.vector.tensor_tensor(out=rb[t][:], in0=b_bank[t // 2][:, t % 2, :], in1=q[:], op=ALU.max)
 
-        def differ(t, dst):
-            y = tile([P, O], F32, "second%d" % t)
-            nc.scalar.activation(out=y[:], in_=rb[t][:].indirect(l5[:]), func=ACT.Copy, scale=sb_t[:, t : t + 1])
-            nc.vector.tensor_tensor(out=dst, in0=rb[t][:].indirect(l4[:]), in1=y[:], op=ALU.subtract)
+        def differ(t, dst, o0=0, o1=O):
+            cols = slice(o0 // 16, o1 // 16)
+            y = tile([P, o1 - o0], F32, "second%d_%d" % (t, o0))
+            nc.scalar.activation(out=y[:], in_=rb[t][:].indirect(l5[:, cols]), func=ACT.Copy, scale=sb_t[:, t : t + 1])
+            nc.vector.tensor_tensor(out=dst[:, o0:o1], in0=rb[t][:].indirect(l4[:, cols]), in1=y[:], op=ALU.subtract)
 
         q0 = fetch(0, None)
         q1 = fetch(1, None)
-        a2 = tile([P, J], F32, "a2_sb", "board0")
+        a2 = tile([P, J], F32, "a2_sb", "a_second_sb")
         nc.vector.tensor_copy(out=a2[:], in_=bank_c[:, 0, :])
         put(2, a2[:], 0, J)
         larger(0, q0)
@@ -195,18 +196,25 @@ def tile_list_ownanswer_twow_store_scattered_kernel(
         low = diff_low[:].rearrange("p t o -> p o t")
         nc.vector.scalar_tensor_tensor(out=hid[:, :, 0:2], in0=low, scalar=-1.0, in1=low, op0=ALU.mult, op1=ALU.max)
 
-        q2 = fetch(2, "second0")
-        q3 = fetch(3, "second1")
+        q2 = fetch(2, "second0_0")
+        q3 = fetch(3, "second1_0")
         larger(2, q2)
         larger(3, q3)
         diff_high = tile([P, 2, O], F32, "diff_high")
         differ(2, diff_high[:, 0, :])
-        differ(3, diff_high[:, 1, :])
-        nc.scalar.activation(out=hid[:, :, 2:4], in_=diff_high[:].rearrange("p t o -> p o t"), func=ACT.Abs)
-
         h_words = tile([P, O], U32, "h_words")
         h_scales = tile([P, O], U8, "h_scales")
-        nc.vector.quantize_mx(out=h_words[:].bitcast(E5M2), scales=h_scales[:], in_=hid[:].rearrange("p o t -> p (o t)"))
+        halves = [(0, O // 2), (O // 2, O)]
+        for o0, o1 in halves:
+            differ(3, diff_high[:, 1, :], o0, o1)
+        for o0, o1 in halves:
+            nc.scalar.activation(
+                out=hid[:, o0:o1, 2:4], in_=diff_high[:, :, o0:o1].rearrange("p t o -> p o t"), func=ACT.Abs
+            )
+            nc.vector.quantize_mx(
+                out=h_words[:, o0:o1].bitcast(E5M2), scales=h_scales[:, o0:o1],
+                in_=hid[:, o0:o1, :].rearrange("p o t -> p (o t)"),
+            )
 
         banks, p_sb = [], []
         for h in range(N // P):

from contextlib import ExitStack

import concourse.mybir as mybir

K, T, J, R, C, O, N, S, E = 512, 1024, 256, 512, 512, 128, 256, 1024, 1024
FLOPS = 2 * (2 * K * R * J + R * N * O)

F32 = mybir.dt.float32
BF16 = mybir.dt.bfloat16
I32 = mybir.dt.int32
U32 = mybir.dt.uint32
U16 = mybir.dt.uint16
U8 = mybir.dt.uint8
E2M1 = mybir.dt.float4_e2m1fn_x4
E4M3 = mybir.dt.float8_e4m3fn_x4
E5M2 = mybir.dt.float8_e5m2_x4
ACT = mybir.ActivationFunctionType
ALU = mybir.AluOpType

P = 128
PACK = 4
QUADS = 4
QROWS = 32
HALF = J // 2


def load_plane(nc, queues, plane, scales):
    rows = scales[0].bitcast(I32)
    nc.vector.memset(plane[:].bitcast(I32), 0)
    for q in range(QUADS):
        queues[q].dma_start(
            out=plane[QROWS * q : QROWS * q + PACK, :].bitcast(I32), in_=rows[PACK * q : PACK * (q + 1), :]
        )


def tile_list_ownanswer_twow_store_scattered_kernel(
    tc, xt_words, xt_scales, w_words, w_scales, w2_words, w2_scales, sa, sb, vs_words, vs_scales,
    offs, offs2, offs3, offs4, offs5, offs6, offs7, out,
):
    nc = tc.nc
    with ExitStack() as ctx:
        lists = ctx.enter_context(tc.tile_pool(name="lists", bufs=1))
        work = ctx.enter_context(tc.tile_pool(name="work", bufs=1))
        psum = ctx.enter_context(tc.psum_pool(name="psum", bufs=1))

        def tile(shape, dtype, name, tag=None):
            return work.tile(shape, dtype, name=name, tag=tag or name, align_bytes=64)

        def load_list(src, name):
            dst = lists.tile(list(src.shape), U16, name=name)
            nc.sync.dma_start(dst[:], src)
            return dst

        def load_words(queue, src, cols, dtype, name):
            dst = tile([P, cols], dtype, name)
            queue.dma_start(out=dst[:].bitcast(I32), in_=src.bitcast(I32))
            return dst

        ws_stage = tile([PACK, QUADS, R // 4], I32, "ws_stage")
        nc.sync.dma_start(out=ws_stage[:], in_=w_scales[0].bitcast(I32).rearrange("(q r) c -> r q c", r=PACK))
        x_words = load_words(nc.scalar, xt_words[0], T, U16, "x_words")
        x_plane = tile([P, T], U8, "x_plane")
        load_plane(nc, [nc.sync, nc.sync, nc.scalar, nc.scalar], x_plane, xt_scales)
        l1 = load_list(offs, "l1")
        w_raw = load_words(nc.scalar, w_words[0].rearrange("p c t -> p (c t)"), R, I32, "w_raw")
        w_plane = tile([P, R], U8, "w_plane")
        nc.vector.memset(w_plane[:].bitcast(I32), 0)
        board = [tile([P, C], F32, "board%d" % t) for t in range(PACK)]
        for t in range(PACK):
            nc.vector.memset(board[t][:], 0.0)
        l2 = load_list(offs2, "l2")
        w2s_stage = tile([PACK, QUADS, R // 4], I32, "w2s_stage")
        nc.sync.dma_start(out=w2s_stage[:], in_=w2_scales[0].bitcast(I32).rearrange("(q r) c -> r q c", r=PACK))
        w2_raw = load_words(nc.sync, w2_words[0].rearrange("p c t -> p (c t)"), R, I32, "w2_raw")
        w2_plane = tile([P, R], U8, "w2_plane")
        nc.vector.memset(w2_plane[:].bitcast(I32), 0)
        l5 = load_list(offs5, "l5")
        sb_t = tile([P, PACK], F32, "sb_t")
        nc.sync.dma_start(out=sb_t[:], in_=sb.rearrange("(p t) o -> p (t o)", t=PACK))
        l3 = load_list(offs3, "l3")
        sa_t = tile([P, PACK], F32, "sa_t")
        nc.sync.dma_start(out=sa_t[:], in_=sa.rearrange("(p t) o -> p (t o)", t=PACK))
        l4 = load_list(offs4, "l4")
        v_words = load_words(nc.sync, vs_words[0].rearrange("p c t -> p (c t)"), S, U32, "v_words")
        l6 = load_list(offs6, "l6")
        v_plane = tile([P, S], U8, "v_plane")
        load_plane(nc, [nc.sync] * QUADS, v_plane, vs_scales)
        l7 = load_list(offs7, "l7")

        for q in range(QUADS):
            nc.vector.tensor_copy(out=w_plane[QROWS * q : QROWS * q + PACK, :].bitcast(I32), in_=ws_stage[:, q, :])

        def deal_scales(plane, name):
            scales = tile([P, PACK, P], U8, name)
            nc.vector.tensor_copy(out=scales[:], in_=plane[:].rearrange("p (m t) -> p t m", t=PACK))
            return scales

        def deal_words(raw, t0, t1, name):
            words = tile([P, t1 - t0, P], I32, name)
            nc.vector.tensor_copy(
                out=words[:].rearrange("p t m -> p m t"),
                in_=raw[:].rearrange("p (m t) -> p m t", t=PACK)[:, :, t0:t1],
            )
            return words

        xg_words = tile([P, J], U16, "xg_words")
        xg_scales = tile([P, J], U8, "xg_scales")

        def pick_tokens(j0, j1):
            cols = l1[:, j0 // 16 : j1 // 16]
            nc.vector.tensor_copy(out=xg_words[:, j0:j1], in_=x_words[:].indirect(cols))
            nc.vector.tensor_copy(out=xg_scales[:, j0:j1], in_=x_plane[:].indirect(cols))

        def stage1(dst, words, scales, fmt, j0, j1):
            nc.tensor.matmul_mx(
                out=dst, lhsT=words.bitcast(fmt), lhsT_scale=scales,
                rhs=xg_words[:, j0:j1].bitcast(E2M1), rhs_scale=xg_scales[:, j0:j1], start=True, stop=True,
            )

        def put(t, src, j0, j1):
            nc.scalar.activation(out=board[t][:].indirect(l2[:, j0 // 16 : j1 // 16]), in_=src, func=ACT.Copy)

        w_sc = deal_scales(w_plane, "w_sc")
        pick_tokens(0, HALF)
        wa_words = deal_words(w_raw, 0, 2, "wa_words")
        first = []
        for t in range(2):
            bank = psum.tile([P, HALF], F32, name="a_first%d" % t)
            stage1(bank[:], wa_words[:, t, :], w_sc[:, t, :], E5M2, 0, HALF)
            a_sb = tile([P, HALF], F32, "a_first_sb%d" % t)
            nc.scalar.activation(out=a_sb[:], in_=bank[:], func=ACT.Copy)
            first.append(a_sb)
        for t in range(2):
            put(t, first[t][:], 0, HALF)

        pick_tokens(HALF, J)
        bank_b = psum.tile([P, 2, HALF], F32, name="a_second")
        for t in range(2):
            stage1(bank_b[:, t, :], wa_words[:, t, :], w_sc[:, t, :], E5M2, HALF, J)
        wb_words = deal_words(w_raw, 2, 4, "wb_words")
        a_second = tile([P, 2, HALF], F32, "a_second_sb")
        nc.vector.tensor_copy(out=a_second[:], in_=bank_b[:])
        for t in range(2):
            put(t, a_second[:, t, :], HALF, J)
        bank_c = psum.tile([P, 2, J], F32, name="a_rest")
        for t in range(2):
            stage1(bank_c[:, t, :], wb_words[:, t, :], w_sc[:, 2 + t, :], E5M2, 0, J)

        for q in range(QUADS):
            nc.vector.tensor_copy(out=w2_plane[QROWS * q : QROWS * q + PACK, :].bitcast(I32), in_=w2s_stage[:, q, :])
        w2_sc = deal_scales(w2_plane, "w2_sc")
        w2d_words = deal_words(w2_raw, 0, PACK, "w2d_words")
        b_bank = [psum.tile([P, 2, J], F32, name="b%d" % u) for u in range(2)]
        for t in range(PACK):
            stage1(b_bank[t // 2][:, t % 2, :], w2d_words[:, t, :], w2_sc[:, t, :], E4M3, 0, J)

        page = [tile([P, E], F32, "page0", "w2_plane"), tile([P, E], F32, "page1", "w2_raw")]
        for h in range(N // P):
            nc.vector.memset(page[h][:], 0.0)
        rb = [tile([P, J], F32, "rb%d" % t) for t in range(PACK)]
        hid = tile([P, O, PACK], BF16, "hid")

        def fetch(t, tag):
            q = tile([P, J], F32, "fetched%d" % t, tag)
            nc.scalar.activation(out=q[:], in_=board[t][:].indirect(l3[:]), func=ACT.Copy, scale=sa_t[:, t : t + 1])
            return q

        def larger(t, q):
            nc.vector.tensor_tensor(out=rb[t][:], in0=b_bank[t // 2][:, t % 2, :], in1=q[:], op=ALU.max)

        def differ(t, dst, o0=0, o1=O):
            cols = slice(o0 // 16, o1 // 16)
            y = tile([P, o1 - o0], F32, "second%d_%d" % (t, o0))
            nc.scalar.activation(out=y[:], in_=rb[t][:].indirect(l5[:, cols]), func=ACT.Copy, scale=sb_t[:, t : t + 1])
            nc.vector.tensor_tensor(out=dst[:, o0:o1], in0=rb[t][:].indirect(l4[:, cols]), in1=y[:], op=ALU.subtract)

        q0 = fetch(0, None)
        q1 = fetch(1, None)
        a2 = tile([P, J], F32, "a2_sb", "a_second_sb")
        nc.vector.tensor_copy(out=a2[:], in_=bank_c[:, 0, :])
        put(2, a2[:], 0, J)
        larger(0, q0)
        larger(1, q1)
        a3 = tile([P, J], F32, "a3_sb", "fetched1")
        nc.vector.tensor_copy(out=a3[:], in_=bank_c[:, 1, :])

        vg_words = tile([P, N], U32, "vg_words")
        vg_scales = tile([P, N], U8, "vg_scales")
        nc.vector.tensor_copy(out=vg_words[:], in_=v_words[:].indirect(l6[:]))
        nc.vector.tensor_copy(out=vg_scales[:], in_=v_plane[:].indirect(l6[:]))

        diff_low = tile([P, 2, O], F32, "diff_low", "v_plane")
        differ(0, diff_low[:, 0, :])
        differ(1, diff_low[:, 1, :])
        put(3, a3[:], 0, J)
        low = diff_low[:].rearrange("p t o -> p o t")
        nc.vector.scalar_tensor_tensor(out=hid[:, :, 0:2], in0=low, scalar=-1.0, in1=low, op0=ALU.mult, op1=ALU.max)

        q2 = fetch(2, "second0_0")
        q3 = fetch(3, "second1_0")
        larger(2, q2)
        larger(3, q3)
        diff_high = tile([P, 2, O], F32, "diff_high")
        differ(2, diff_high[:, 0, :])
        h_words = tile([P, O], U32, "h_words")
        h_scales = tile([P, O], U8, "h_scales")
        halves = [(0, O // 2), (O // 2, O)]
        for o0, o1 in halves:
            differ(3, diff_high[:, 1, :], o0, o1)
        for o0, o1 in halves:
            nc.scalar.activation(
                out=hid[:, o0:o1, 2:4], in_=diff_high[:, :, o0:o1].rearrange("p t o -> p o t"), func=ACT.Abs
            )
            nc.vector.quantize_mx(
                out=h_words[:, o0:o1].bitcast(E5M2), scales=h_scales[:, o0:o1],
                in_=hid[:, o0:o1, :].rearrange("p o t -> p (o t)"),
            )

        banks, p_sb = [], []
        for h in range(N // P):
            bank = psum.tile([P, O], F32, name="p%d" % h)
            nc.tensor.matmul_mx(
                out=bank[:], lhsT=vg_words[:, h * P : (h + 1) * P].bitcast(E4M3), lhsT_scale=vg_scales[:, h * P : (h + 1) * P],
                rhs=h_words[:].bitcast(E5M2), rhs_scale=h_scales[:], start=True, stop=True,
            )
            banks.append(bank)
            p_sb.append(tile([P, O], F32, "p_sb%d" % h))
        nc.scalar.activation(out=p_sb[0][:], in_=banks[0][:], func=ACT.Copy)
        nc.vector.tensor_copy(out=p_sb[1][:], in_=banks[1][:])
        nc.vector.tensor_copy(out=page[0][:].indirect(l7[:]), in_=p_sb[0][:])
        nc.scalar.activation(out=page[1][:].indirect(l7[:]), in_=p_sb[1][:], func=ACT.Copy)
        for h in range(N // P):
            nc.sync.dma_start(out=out[h * P : (h + 1) * P, :], in_=page[h][:])
